import numpy as np
CORES = [9,41,49,65,73,81,97,113,15,47,55,71,79,87,103,119]
N = 16
TIMES = 2
def setup_inputs(rng):
    x = (rng.standard_normal((N, 128, 128), dtype=np.float32) / np.float32(np.sqrt(512 * N)))
    return {"x": x, "xt": x.transpose(0, 2, 1).copy()}
def setup_inputs_big(rng):
    d = setup_inputs(rng)
    for k in ("x", "xt"): d[k] = (d[k].astype(np.float32) * 1024.0).astype(d[k].dtype)
    return d
def setup_inputs_small(rng):
    d = setup_inputs(rng)
    for k in ("x", "xt"): d[k] = (d[k].astype(np.float32) * (1 / 1024.0)).astype(d[k].dtype)
    return d
def setup_inputs_apart(rng):
    d = setup_inputs(rng)
    f = (10.0 ** rng.permutation(np.linspace(-1.5, 1.5, N))).astype(np.float32).reshape(N, 1, 1)
    for k in ("x", "xt"): d[k] = (d[k].astype(np.float32) * f).astype(d[k].dtype)
    return d
def reference(x, xt):
    X = list(x.astype(np.float64))
    for _ in range(TIMES):
        G = sum(a.T @ a for a in X)
        X = [1.5 * a - 0.5 * (a @ G) for a in X]
    return {"y": np.stack(X).astype(np.float32)}

@@ -1,0 +1,171 @@
+from concourse.bass import DstId, RemoteDMATransfer
+from concourse.mybir import AluOpType
+
+HALF = 64
+R1_ENGINES = 8
+R3_ENGINES = 16
+
+SCRATCH = {
+    "xs": ("sbuf", [128, 128], "float32"),
+    "xts": ("sbuf", [128, 128], "float32"),
+    "cm05": ("sbuf", [128, 128], "float32"),
+    "c15": ("sbuf", [128, 128], "float32"),
+    "gs": ("sbuf", [128, 128], "float32"),
+    "xt15": ("sbuf", [128, 128], "float32"),
+    "p": ("sbuf", [128, 128], "float32"),
+    "qs": ("sbuf", [128, 128], "float32"),
+    "dt": ("sbuf", [128, 128], "float32"),
+    "ws": ("sbuf", [128, 128], "float32"),
+    "ys": ("sbuf", [128, 128], "float32"),
+    "pg": ("psum", [128, 512], "float32"),
+    "pq": ("psum", [128, 512], "float32"),
+    "pt": ("psum", [128, 512], "float32"),
+    "pw": ("psum", [128, 512], "float32"),
+    "py": ("psum", [128, 512], "float32"),
+    "pat": ("sbuf", [128, HALF + 1], "float32"),
+    "zero": ("sbuf", [128, HALF], "float32"),
+    "part": ("dram", [2, 128, HALF], "float32"),
+    "land": ("dram", [8, 128, HALF], "float32"),
+    "diag": ("dram", [129, HALF], "float32"),
+}
+SEMAPHORES = ["s_x", "s_xt", "s_c1", "s_c2", "s_g", "s_gs", "s_x15", "s_p", "s_q", "s_t", "s_qs", "s_dt", "s_w",
+              "s_ws", "s_y", "s_ys", "s_st", "s_sent", "a_fill", "a_d1", "a_d2", "a_part", "a_land", "a_sent"]
+
+
+def _bits(m):
+    return [1 << i for i in range(m.bit_length()) if (m >> i) & 1]
+
+
+def _join(bits):
+    m = 0
+    for b in bits:
+        m |= b
+    return m
+
+
+def _plan(T, topo):
+    cores = list(T.cores)
+    chips = sorted({topo.chip(c) for c in cores})
+    ranks = {ch: [c for c in cores if topo.chip(c) == ch] for ch in chips}
+    span = range(0, max(cores) + 64)
+    agents = {}
+    for ch in chips:
+        for c in span:
+            if topo.chip(c) != ch or c in cores:
+                continue
+            if all(topo.may_write(c, r) for r in cores):
+                agents.setdefault((ch, topo.die(c)), c)
+    dies = sorted({d for (_, d) in agents})
+    return chips, ranks, agents, dies
+
+
+def _dst(topo, c):
+    rid, pid, _ = topo.addr(c)
+    return DstId(rid=rid, pnc=pid)
+
+
+def _rank(g, core, T, topo, chips, ranks, agents, dies):
+    S = T.sem
+    ch = topo.chip(core)
+    slot = ranks[ch].index(core)
+    A = slice(0, 128)
+
+    g.sync.dma_start(T.xs[:], T.x[:]).then_inc(S.s_x, 16)
+    g.scalar.dma_start(T.xts[:], T.xt[:]).then_inc(S.s_xt, 16)
+    g.vector.memset(T.cm05[:], -0.5).then_inc(S.s_c1, 1)
+    g.vector.memset(T.c15[:], 1.5).then_inc(S.s_c2, 1)
+
+    g.tensor.wait_ge(S.s_x, 16)
+    g.tensor.matmul(T.pg[:, A], T.xs[:], T.xs[:], True, True).then_inc(S.s_g, 1)
+    g.vector.wait_ge(S.s_c1, 1)
+    g.vector.wait_ge(S.s_g, 1)
+    g.vector.tensor_tensor(T.gs[:], T.pg[:, A], T.cm05[:], AluOpType.mult).then_inc(S.s_gs, 1)
+
+    mine = [agents[(ch, d)] for d in dies]
+    common = topo.mask(core, mine[0]) & topo.mask(core, mine[1])
+    b = _bits(common)
+    lanes = [b[0::2][:R1_ENGINES], b[1::2][:R1_ENGINES]]
+    g.wait_ge(S.s_gs, 1)
+    g.remote_dma_fused(
+        [RemoteDMATransfer(dst_ids=[_dst(topo, mine[u])], dma_engine_mask=_join(lanes[u]), remote_sem=S.a_part,
+                           src=T.gs[:, HALF * u:HALF * (u + 1)], dst=T.part[slot]) for u in range(2)],
+        local_sem=S.s_sent)
+
+    g.vector.wait_ge(S.s_c2, 1)
+    g.vector.wait_ge(S.s_xt, 16)
+    g.vector.tensor_tensor(T.xt15[:], T.xts[:], T.c15[:], AluOpType.mult).then_inc(S.s_x15, 1)
+
+    g.tensor.wait_ge(S.s_xt, 16)
+    g.tensor.wait_ge(S.s_p, 2 * R3_ENGINES)
+    g.tensor.matmul(T.pq[:, A], T.p[:], T.p[:], True, True).then_inc(S.s_q, 1)
+    g.tensor.matmul(T.pt[:, A], T.p[:], T.xts[:], True, True).then_inc(S.s_t, 1)
+    g.vector.wait_ge(S.s_q, 1)
+    g.vector.tensor_copy(T.qs[:], T.pq[:, A]).then_inc(S.s_qs, 1)
+    g.vector.wait_ge(S.s_x15, 1)
+    g.vector.wait_ge(S.s_t, 1)
+    g.vector.tensor_tensor(T.dt[:], T.pt[:, A], T.xt15[:], AluOpType.subtract).then_inc(S.s_dt, 1)
+    g.tensor.wait_ge(S.s_qs, 1)
+    g.tensor.matmul(T.pw[:, A], T.qs[:], T.p[:], True, True).then_inc(S.s_w, 1)
+    g.tensor.wait_ge(S.s_x15, 1)
+    g.tensor.matmul(T.py[:, A], T.xt15[:], T.p[:], True, False)
+    g.vector.wait_ge(S.s_w, 1)
+    g.vector.tensor_copy(T.ws[:], T.pw[:, A]).then_inc(S.s_ws, 1)
+    g.tensor.wait_ge(S.s_dt, 1)
+    g.tensor.wait_ge(S.s_ws, 1)
+    g.tensor.matmul(T.py[:, A], T.dt[:], T.ws[:], False, True).then_inc(S.s_y, 1)
+    g.vector.wait_ge(S.s_y, 1)
+    g.vector.tensor_copy(T.ys[:], T.py[:, A]).then_inc(S.s_ys, 1)
+    g.sync.wait_ge(S.s_ys, 1)
+    g.sync.dma_start(T.y[:], T.ys[:]).then_inc(S.s_st, 16)
+    g.sync.wait_ge(S.s_st, 16)
+    g.wait_ge(S.s_sent, 2 * R1_ENGINES)
+
+
+def _agent(g, core, T, topo, chips, ranks, agents, dies):
+    S = T.sem
+    ch = topo.chip(core)
+    die = topo.die(core)
+    u = dies.index(die)
+    ci = chips.index(ch)
+
+    g.vector.memset(T.pat[0:HALF, 0:1], 1.5).then_inc(S.a_fill, 1)
+    g.vector.memset(T.pat[0:HALF, 1:HALF + 1], 0.0).then_inc(S.a_fill, 1)
+    g.vector.memset(T.zero[:], 0.0).then_inc(S.a_fill, 1)
+    base = HALF * u
+    g.sync.wait_ge(S.a_fill, 3)
+    g.sync.dma_start(T.diag[base:base + HALF + 1, :], T.pat[0:HALF, :]).then_inc(S.a_d1, 16)
+    lo, hi = (0, base) if u else (HALF + 1, 128)
+    g.scalar.wait_ge(S.a_fill, 3)
+    g.scalar.dma_start(T.diag[lo:hi, :], T.zero[0:hi - lo, :]).then_inc(S.a_d2, 16)
+
+    peers = [agents[(c, die)] for c in chips if c != ch]
+    m = topo.mask(core, peers[0])
+    for p in peers:
+        m &= topo.mask(core, p)
+    n2 = len(_bits(m))
+    g.wait_ge(S.a_part, 2 * R1_ENGINES)
+    g.remote_dma_fused(
+        [RemoteDMATransfer(dst_ids=[_dst(topo, p) for p in peers], dma_engine_mask=m, remote_sem=S.a_land,
+                           srcs=[T.part[0], T.part[1]], dsts=[T.land[ci] for _ in peers], alu_op=1)],
+        local_sem=S.a_sent)
+
+    here = ranks[ch]
+    m3 = topo.mask(core, here[0]) & topo.mask(core, here[1])
+    m3 = _join(_bits(m3)[:R3_ENGINES])
+    srcs = [T.land[k] for k in range(len(chips)) if k != ci] + [T.part[0], T.part[1], T.diag[0:128, :]]
+    g.wait_ge(S.a_d1, 16)
+    g.wait_ge(S.a_d2, 16)
+    g.wait_ge(S.a_land, n2 * len(peers))
+    g.remote_dma_fused(
+        [RemoteDMATransfer(dst_ids=[_dst(topo, r) for r in here], dma_engine_mask=m3, remote_sem=S.s_p,
+                           srcs=srcs, dsts=[T.p[:, HALF * u:HALF * (u + 1)] for _ in here], alu_op=1)],
+        local_sem=S.a_sent)
+    g.wait_ge(S.a_sent, n2 + R3_ENGINES)
+
+
+def rank_program(g, core, T, topo):
+    chips, ranks, agents, dies = _plan(T, topo)
+    if T.rank_of(core) is not None:
+        _rank(g, core, T, topo, chips, ranks, agents, dies)
+    elif core in agents.values():
+        _agent(g, core, T, topo, chips, ranks, agents, dies)

@@ -2,6 +2,7 @@ from concourse.bass import DstId, RemoteDMATransfer
 from concourse.mybir import AluOpType
 
 HALF = 64
+R0_ENGINES = 16
 R1_ENGINES = 8
 R3_ENGINES = 16
 
@@ -9,18 +10,18 @@ SCRATCH = {
     "xs": ("sbuf", [128, 128], "float32"),
     "xts": ("sbuf", [128, 128], "float32"),
     "cm05": ("sbuf", [128, 128], "float32"),
-    "c15": ("sbuf", [128, 128], "float32"),
     "gs": ("sbuf", [128, 128], "float32"),
-    "xt15": ("sbuf", [128, 128], "float32"),
+    "i15": ("sbuf", [128, 128], "float32"),
     "p": ("sbuf", [128, 128], "float32"),
+    "h": ("sbuf", [128, 128], "float32"),
     "qs": ("sbuf", [128, 128], "float32"),
-    "dt": ("sbuf", [128, 128], "float32"),
-    "ws": ("sbuf", [128, 128], "float32"),
+    "x1t": ("sbuf", [128, 128], "float32"),
+    "ss": ("sbuf", [128, 128], "float32"),
     "ys": ("sbuf", [128, 128], "float32"),
     "pg": ("psum", [128, 512], "float32"),
     "pq": ("psum", [128, 512], "float32"),
     "pt": ("psum", [128, 512], "float32"),
-    "pw": ("psum", [128, 512], "float32"),
+    "pr": ("psum", [128, 512], "float32"),
     "py": ("psum", [128, 512], "float32"),
     "pat": ("sbuf", [128, HALF + 1], "float32"),
     "zero": ("sbuf", [128, HALF], "float32"),
@@ -28,8 +29,8 @@ SCRATCH = {
     "land": ("dram", [8, 128, HALF], "float32"),
     "diag": ("dram", [129, HALF], "float32"),
 }
-SEMAPHORES = ["s_x", "s_xt", "s_c1", "s_c2", "s_g", "s_gs", "s_x15", "s_p", "s_q", "s_t", "s_qs", "s_dt", "s_w",
-              "s_ws", "s_y", "s_ys", "s_st", "s_sent", "a_fill", "a_d1", "a_d2", "a_part", "a_land", "a_sent"]
+SEMAPHORES = ["s_x", "s_xt", "s_c1", "s_g", "s_gs", "s_i", "s_p", "s_h", "s_q", "s_t", "s_qs", "s_x1", "s_r",
+              "s_ss", "s_y", "s_ys", "s_st", "s_sent", "a_fill", "a_d1", "a_d2", "a_part", "a_land", "a_sent"]
 
 
 def _bits(m):
@@ -73,7 +74,6 @@ def _rank(g, core, T, topo, chips, ranks, agents, dies):
     g.sync.dma_start(T.xs[:], T.x[:]).then_inc(S.s_x, 16)
     g.scalar.dma_start(T.xts[:], T.xt[:]).then_inc(S.s_xt, 16)
     g.vector.memset(T.cm05[:], -0.5).then_inc(S.s_c1, 1)
-    g.vector.memset(T.c15[:], 1.5).then_inc(S.s_c2, 1)
 
     g.tensor.wait_ge(S.s_x, 16)
     g.tensor.matmul(T.pg[:, A], T.xs[:], T.xs[:], True, True).then_inc(S.s_g, 1)
@@ -91,28 +91,25 @@ def _rank(g, core, T, topo, chips, ranks, agents, dies):
                            src=T.gs[:, HALF * u:HALF * (u + 1)], dst=T.part[slot]) for u in range(2)],
         local_sem=S.s_sent)
 
-    g.vector.wait_ge(S.s_c2, 1)
-    g.vector.wait_ge(S.s_xt, 16)
-    g.vector.tensor_tensor(T.xt15[:], T.xts[:], T.c15[:], AluOpType.mult).then_inc(S.s_x15, 1)
-
     g.tensor.wait_ge(S.s_xt, 16)
     g.tensor.wait_ge(S.s_p, 2 * R3_ENGINES)
     g.tensor.matmul(T.pq[:, A], T.p[:], T.p[:], True, True).then_inc(S.s_q, 1)
     g.tensor.matmul(T.pt[:, A], T.p[:], T.xts[:], True, True).then_inc(S.s_t, 1)
+    g.vector.wait_ge(S.s_i, 2 * R0_ENGINES)
+    g.vector.wait_ge(S.s_p, 2 * R3_ENGINES)
+    g.vector.tensor_tensor(T.h[:], T.p[:], T.i15[:], AluOpType.subtract).then_inc(S.s_h, 1)
     g.vector.wait_ge(S.s_q, 1)
     g.vector.tensor_copy(T.qs[:], T.pq[:, A]).then_inc(S.s_qs, 1)
-    g.vector.wait_ge(S.s_x15, 1)
     g.vector.wait_ge(S.s_t, 1)
-    g.vector.tensor_tensor(T.dt[:], T.pt[:, A], T.xt15[:], AluOpType.subtract).then_inc(S.s_dt, 1)
+    g.vector.tensor_copy(T.x1t[:], T.pt[:, A]).then_inc(S.s_x1, 1)
+    g.tensor.wait_ge(S.s_h, 1)
     g.tensor.wait_ge(S.s_qs, 1)
-    g.tensor.matmul(T.pw[:, A], T.qs[:], T.p[:], True, True).then_inc(S.s_w, 1)
-    g.tensor.wait_ge(S.s_x15, 1)
-    g.tensor.matmul(T.py[:, A], T.xt15[:], T.p[:], True, False)
-    g.vector.wait_ge(S.s_w, 1)
-    g.vector.tensor_copy(T.ws[:], T.pw[:, A]).then_inc(S.s_ws, 1)
-    g.tensor.wait_ge(S.s_dt, 1)
-    g.tensor.wait_ge(S.s_ws, 1)
-    g.tensor.matmul(T.py[:, A], T.dt[:], T.ws[:], False, True).then_inc(S.s_y, 1)
+    g.tensor.matmul(T.pr[:, A], T.qs[:], T.h[:], True, True).then_inc(S.s_r, 1)
+    g.vector.wait_ge(S.s_r, 1)
+    g.vector.tensor_tensor(T.ss[:], T.pr[:, A], T.i15[:], AluOpType.add).then_inc(S.s_ss, 1)
+    g.tensor.wait_ge(S.s_x1, 1)
+    g.tensor.wait_ge(S.s_ss, 1)
+    g.tensor.matmul(T.py[:, A], T.x1t[:], T.ss[:], True, True).then_inc(S.s_y, 1)
     g.vector.wait_ge(S.s_y, 1)
     g.vector.tensor_copy(T.ys[:], T.py[:, A]).then_inc(S.s_ys, 1)
     g.sync.wait_ge(S.s_ys, 1)
@@ -127,6 +124,9 @@ def _agent(g, core, T, topo, chips, ranks, agents, dies):
     die = topo.die(core)
     u = dies.index(die)
     ci = chips.index(ch)
+    here = ranks[ch]
+    cols = slice(HALF * u, HALF * (u + 1))
+    onchip = _bits(topo.mask(core, here[0]) & topo.mask(core, here[1]))
 
     g.vector.memset(T.pat[0:HALF, 0:1], 1.5).then_inc(S.a_fill, 1)
     g.vector.memset(T.pat[0:HALF, 1:HALF + 1], 0.0).then_inc(S.a_fill, 1)
@@ -137,6 +137,13 @@ def _agent(g, core, T, topo, chips, ranks, agents, dies):
     lo, hi = (0, base) if u else (HALF + 1, 128)
     g.scalar.wait_ge(S.a_fill, 3)
     g.scalar.dma_start(T.diag[lo:hi, :], T.zero[0:hi - lo, :]).then_inc(S.a_d2, 16)
+
+    g.wait_ge(S.a_d1, 16)
+    g.wait_ge(S.a_d2, 16)
+    g.remote_dma_fused(
+        [RemoteDMATransfer(dst_ids=[_dst(topo, r) for r in here], dma_engine_mask=_join(onchip[:R0_ENGINES]),
+                           remote_sem=S.s_i, src=T.diag[0:128, :], dsts=[T.i15[:, cols] for _ in here])],
+        local_sem=S.a_sent)
 
     peers = [agents[(c, die)] for c in chips if c != ch]
     m = topo.mask(core, peers[0])
@@ -149,18 +156,13 @@ def _agent(g, core, T, topo, chips, ranks, agents, dies):
                            srcs=[T.part[0], T.part[1]], dsts=[T.land[ci] for _ in peers], alu_op=1)],
         local_sem=S.a_sent)
 
-    here = ranks[ch]
-    m3 = topo.mask(core, here[0]) & topo.mask(core, here[1])
-    m3 = _join(_bits(m3)[:R3_ENGINES])
     srcs = [T.land[k] for k in range(len(chips)) if k != ci] + [T.part[0], T.part[1], T.diag[0:128, :]]
-    g.wait_ge(S.a_d1, 16)
-    g.wait_ge(S.a_d2, 16)
     g.wait_ge(S.a_land, n2 * len(peers))
     g.remote_dma_fused(
-        [RemoteDMATransfer(dst_ids=[_dst(topo, r) for r in here], dma_engine_mask=m3, remote_sem=S.s_p,
-                           srcs=srcs, dsts=[T.p[:, HALF * u:HALF * (u + 1)] for _ in here], alu_op=1)],
+        [RemoteDMATransfer(dst_ids=[_dst(topo, r) for r in here], dma_engine_mask=_join(onchip[:R3_ENGINES]),
+                           remote_sem=S.s_p, srcs=srcs, dsts=[T.p[:, cols] for _ in here], alu_op=1)],
         local_sem=S.a_sent)
-    g.wait_ge(S.a_sent, n2 + R3_ENGINES)
+    g.wait_ge(S.a_sent, R0_ENGINES + n2 + R3_ENGINES)
 
 
 def rank_program(g, core, T, topo):

@@ -2,14 +2,12 @@ from concourse.bass import DstId, RemoteDMATransfer
 from concourse.mybir import AluOpType
 
 HALF = 64
-R0_ENGINES = 16
-R1_ENGINES = 8
-R3_ENGINES = 16
+ON = 16
 
 SCRATCH = {
     "xs": ("sbuf", [128, 128], "float32"),
     "xts": ("sbuf", [128, 128], "float32"),
-    "cm05": ("sbuf", [128, 128], "float32"),
+    "cm05": ("sbuf", [128, HALF], "float32"),
     "gs": ("sbuf", [128, 128], "float32"),
     "i15": ("sbuf", [128, 128], "float32"),
     "p": ("sbuf", [128, 128], "float32"),
@@ -18,19 +16,22 @@ SCRATCH = {
     "x1t": ("sbuf", [128, 128], "float32"),
     "ss": ("sbuf", [128, 128], "float32"),
     "ys": ("sbuf", [128, 128], "float32"),
-    "pg": ("psum", [128, 512], "float32"),
+    "pg0": ("psum", [128, 512], "float32"),
+    "pg1": ("psum", [128, 512], "float32"),
     "pq": ("psum", [128, 512], "float32"),
     "pt": ("psum", [128, 512], "float32"),
     "pr": ("psum", [128, 512], "float32"),
-    "py": ("psum", [128, 512], "float32"),
+    "py0": ("psum", [128, 512], "float32"),
+    "py1": ("psum", [128, 512], "float32"),
     "pat": ("sbuf", [128, HALF + 1], "float32"),
     "zero": ("sbuf", [128, HALF], "float32"),
     "part": ("dram", [2, 128, HALF], "float32"),
     "land": ("dram", [8, 128, HALF], "float32"),
     "diag": ("dram", [129, HALF], "float32"),
 }
-SEMAPHORES = ["s_x", "s_xt", "s_c1", "s_g", "s_gs", "s_i", "s_p", "s_h", "s_q", "s_t", "s_qs", "s_x1", "s_r",
-              "s_ss", "s_y", "s_ys", "s_st", "s_sent", "a_fill", "a_d1", "a_d2", "a_part", "a_land", "a_sent"]
+SEMAPHORES = ["s_x", "s_xt", "s_c1", "s_g0", "s_g1", "s_gs0", "s_gs1", "s_i", "s_p", "s_h", "s_q", "s_t", "s_qs",
+              "s_x1", "s_r", "s_ss0", "s_ss1", "s_y0", "s_y1", "s_ys0", "s_ys1", "s_st0", "s_st1", "s_sent",
+              "s_own", "a_fill", "a_d1", "a_d2", "a_part", "a_land", "a_sent"]
 
 
 def _bits(m):
@@ -44,20 +45,28 @@ def _join(bits):
     return m
 
 
+def _mask(topo, src, dsts, n=None):
+    m = topo.mask(src, dsts[0])
+    for d in dsts:
+        m &= topo.mask(src, d)
+    b = _bits(m)
+    return _join(b if n is None else b[:n])
+
+
 def _plan(T, topo):
     cores = list(T.cores)
     chips = sorted({topo.chip(c) for c in cores})
     ranks = {ch: [c for c in cores if topo.chip(c) == ch] for ch in chips}
-    span = range(0, max(cores) + 64)
-    agents = {}
-    for ch in chips:
-        for c in span:
-            if topo.chip(c) != ch or c in cores:
-                continue
-            if all(topo.may_write(c, r) for r in cores):
-                agents.setdefault((ch, topo.die(c)), c)
+    able = {}
+    for c in range(0, max(cores) + 64):
+        if topo.chip(c) in ranks and all(topo.may_write(c, r) for r in cores if r != c):
+            able.setdefault((topo.chip(c), topo.die(c)), []).append(c)
+    agents, seconds = {}, {}
+    for key, cs in able.items():
+        order = [c for c in cs if c not in cores] + [c for c in cs if c in cores]
+        agents[key], seconds[key] = order[0], order[1]
     dies = sorted({d for (_, d) in agents})
-    return chips, ranks, agents, dies
+    return chips, ranks, agents, seconds, dies
 
 
 def _dst(topo, c):
@@ -65,38 +74,62 @@ def _dst(topo, c):
     return DstId(rid=rid, pnc=pid)
 
 
-def _rank(g, core, T, topo, chips, ranks, agents, dies):
+def _spread(g, core, T, topo, plan, second, local_sem):
+    chips, ranks, agents, seconds, dies = plan
+    ch = topo.chip(core)
+    peers = [agents[(c, topo.die(core))] for c in chips if c != ch][(1 if second else 0)::2]
+    m = _mask(topo, core, peers)
+    g.remote_dma_fused(
+        [RemoteDMATransfer(dst_ids=[_dst(topo, p) for p in peers], dma_engine_mask=m, remote_sem=T.sem.a_land,
+                           srcs=[T.part[0], T.part[1]], dsts=[T.land[chips.index(ch)] for _ in peers], alu_op=1)],
+        local_sem=local_sem)
+    return len(_bits(m))
+
+
+def _rank(g, core, T, topo, plan):
+    chips, ranks, agents, seconds, dies = plan
     S = T.sem
     ch = topo.chip(core)
     slot = ranks[ch].index(core)
     A = slice(0, 128)
+    B = slice(0, HALF)
+    cols = [slice(HALF * u, HALF * (u + 1)) for u in range(2)]
+    sender = seconds[(ch, topo.die(core))] == core
 
     g.sync.dma_start(T.xs[:], T.x[:]).then_inc(S.s_x, 16)
+    g.scalar.wait_ge(S.s_x, 16)
     g.scalar.dma_start(T.xts[:], T.xt[:]).then_inc(S.s_xt, 16)
     g.vector.memset(T.cm05[:], -0.5).then_inc(S.s_c1, 1)
 
     g.tensor.wait_ge(S.s_x, 16)
-    g.tensor.matmul(T.pg[:, A], T.xs[:], T.xs[:], True, True).then_inc(S.s_g, 1)
     g.vector.wait_ge(S.s_c1, 1)
-    g.vector.wait_ge(S.s_g, 1)
-    g.vector.tensor_tensor(T.gs[:], T.pg[:, A], T.cm05[:], AluOpType.mult).then_inc(S.s_gs, 1)
-
-    mine = [agents[(ch, d)] for d in dies]
-    common = topo.mask(core, mine[0]) & topo.mask(core, mine[1])
-    b = _bits(common)
-    lanes = [b[0::2][:R1_ENGINES], b[1::2][:R1_ENGINES]]
-    g.wait_ge(S.s_gs, 1)
-    g.remote_dma_fused(
-        [RemoteDMATransfer(dst_ids=[_dst(topo, mine[u])], dma_engine_mask=_join(lanes[u]), remote_sem=S.a_part,
-                           src=T.gs[:, HALF * u:HALF * (u + 1)], dst=T.part[slot]) for u in range(2)],
-        local_sem=S.s_sent)
+    for u in range(2):
+        pg = T["pg%d" % u]
+        key = (ch, dies[u])
+        to = [c for c in (agents[key], seconds[key]) if c != core]
+        g.tensor.matmul(pg[:, B], T.xs[:], T.xs[:, cols[u]], True, True).then_inc(S["s_g%d" % u], 1)
+        g.vector.wait_ge(S["s_g%d" % u], 1)
+        g.vector.tensor_tensor(T.gs[:, cols[u]], pg[:, B], T.cm05[:], AluOpType.mult).then_inc(S["s_gs%d" % u], 1)
+        g.wait_ge(S["s_gs%d" % u], 1)
+        g.remote_dma_fused(
+            [RemoteDMATransfer(dst_ids=[_dst(topo, c) for c in to], dma_engine_mask=_mask(topo, core, to, ON),
+                               remote_sem=S.a_part, src=T.gs[:, cols[u]], dsts=[T.part[slot] for _ in to])],
+            local_sem=S.s_sent)
+        if len(to) == 1:
+            g.sync.wait_ge(S["s_gs%d" % u], 1)
+            g.sync.dma_start(T.part[slot], T.gs[:, cols[u]]).then_inc(S.s_own, 16)
+    sent = 2 * ON
+    if sender:
+        g.wait_ge(S.s_own, 16)
+        g.wait_ge(S.a_part, ON)
+        sent += _spread(g, core, T, topo, plan, True, S.s_sent)
 
     g.tensor.wait_ge(S.s_xt, 16)
-    g.tensor.wait_ge(S.s_p, 2 * R3_ENGINES)
+    g.tensor.wait_ge(S.s_p, 2 * ON)
     g.tensor.matmul(T.pq[:, A], T.p[:], T.p[:], True, True).then_inc(S.s_q, 1)
     g.tensor.matmul(T.pt[:, A], T.p[:], T.xts[:], True, True).then_inc(S.s_t, 1)
-    g.vector.wait_ge(S.s_i, 2 * R0_ENGINES)
-    g.vector.wait_ge(S.s_p, 2 * R3_ENGINES)
+    g.vector.wait_ge(S.s_i, 2 * ON)
+    g.vector.wait_ge(S.s_p, 2 * ON)
     g.vector.tensor_tensor(T.h[:], T.p[:], T.i15[:], AluOpType.subtract).then_inc(S.s_h, 1)
     g.vector.wait_ge(S.s_q, 1)
     g.vector.tensor_copy(T.qs[:], T.pq[:, A]).then_inc(S.s_qs, 1)
@@ -106,27 +139,33 @@ def _rank(g, core, T, topo, chips, ranks, agents, dies):
     g.tensor.wait_ge(S.s_qs, 1)
     g.tensor.matmul(T.pr[:, A], T.qs[:], T.h[:], True, True).then_inc(S.s_r, 1)
     g.vector.wait_ge(S.s_r, 1)
-    g.vector.tensor_tensor(T.ss[:], T.pr[:, A], T.i15[:], AluOpType.add).then_inc(S.s_ss, 1)
+    for u in range(2):
+        g.vector.tensor_tensor(T.ss[:, cols[u]], T.pr[:, cols[u]], T.i15[:, cols[u]],
+                               AluOpType.add).then_inc(S["s_ss%d" % u], 1)
     g.tensor.wait_ge(S.s_x1, 1)
-    g.tensor.wait_ge(S.s_ss, 1)
-    g.tensor.matmul(T.py[:, A], T.x1t[:], T.ss[:], True, True).then_inc(S.s_y, 1)
-    g.vector.wait_ge(S.s_y, 1)
-    g.vector.tensor_copy(T.ys[:], T.py[:, A]).then_inc(S.s_ys, 1)
-    g.sync.wait_ge(S.s_ys, 1)
-    g.sync.dma_start(T.y[:], T.ys[:]).then_inc(S.s_st, 16)
-    g.sync.wait_ge(S.s_st, 16)
-    g.wait_ge(S.s_sent, 2 * R1_ENGINES)
+    queues = [g.sync, g.scalar]
+    for u in range(2):
+        py = T["py%d" % u]
+        g.tensor.wait_ge(S["s_ss%d" % u], 1)
+        g.tensor.matmul(py[:, B], T.x1t[:], T.ss[:, cols[u]], True, True).then_inc(S["s_y%d" % u], 1)
+        g.vector.wait_ge(S["s_y%d" % u], 1)
+        g.vector.tensor_copy(T.ys[:, cols[u]], py[:, B]).then_inc(S["s_ys%d" % u], 1)
+        queues[u].wait_ge(S["s_ys%d" % u], 1)
+        queues[u].dma_start(T.y[:, cols[u]], T.ys[:, cols[u]]).then_inc(S["s_st%d" % u], 16)
+        queues[u].wait_ge(S["s_st%d" % u], 16)
+    g.wait_ge(S.s_sent, sent)
 
 
-def _agent(g, core, T, topo, chips, ranks, agents, dies):
+def _helper(g, core, T, topo, plan):
+    chips, ranks, agents, seconds, dies = plan
     S = T.sem
     ch = topo.chip(core)
-    die = topo.die(core)
-    u = dies.index(die)
+    key = (ch, topo.die(core))
+    u = dies.index(key[1])
     ci = chips.index(ch)
     here = ranks[ch]
+    second = seconds[key] == core
     cols = slice(HALF * u, HALF * (u + 1))
-    onchip = _bits(topo.mask(core, here[0]) & topo.mask(core, here[1]))
 
     g.vector.memset(T.pat[0:HALF, 0:1], 1.5).then_inc(S.a_fill, 1)
     g.vector.memset(T.pat[0:HALF, 1:HALF + 1], 0.0).then_inc(S.a_fill, 1)
@@ -138,36 +177,35 @@ def _agent(g, core, T, topo, chips, ranks, agents, dies):
     g.scalar.wait_ge(S.a_fill, 3)
     g.scalar.dma_start(T.diag[lo:hi, :], T.zero[0:hi - lo, :]).then_inc(S.a_d2, 16)
 
+    if seconds[key] in here:
+        to = here
+    else:
+        to = here[1:] if second else here[:1]
     g.wait_ge(S.a_d1, 16)
     g.wait_ge(S.a_d2, 16)
     g.remote_dma_fused(
-        [RemoteDMATransfer(dst_ids=[_dst(topo, r) for r in here], dma_engine_mask=_join(onchip[:R0_ENGINES]),
-                           remote_sem=S.s_i, src=T.diag[0:128, :], dsts=[T.i15[:, cols] for _ in here])],
+        [RemoteDMATransfer(dst_ids=[_dst(topo, r) for r in to], dma_engine_mask=_mask(topo, core, here, ON),
+                           remote_sem=S.s_i, src=T.diag[0:128, :], dsts=[T.i15[:, cols] for _ in to])],
         local_sem=S.a_sent)
 
-    peers = [agents[(c, die)] for c in chips if c != ch]
-    m = topo.mask(core, peers[0])
-    for p in peers:
-        m &= topo.mask(core, p)
-    n2 = len(_bits(m))
-    g.wait_ge(S.a_part, 2 * R1_ENGINES)
-    g.remote_dma_fused(
-        [RemoteDMATransfer(dst_ids=[_dst(topo, p) for p in peers], dma_engine_mask=m, remote_sem=S.a_land,
-                           srcs=[T.part[0], T.part[1]], dsts=[T.land[ci] for _ in peers], alu_op=1)],
-        local_sem=S.a_sent)
+    g.wait_ge(S.a_part, 2 * ON)
+    n2 = _spread(g, core, T, topo, plan, second, S.a_sent)
+    if second:
+        g.wait_ge(S.a_sent, ON + n2)
+        return
 
     srcs = [T.land[k] for k in range(len(chips)) if k != ci] + [T.part[0], T.part[1], T.diag[0:128, :]]
-    g.wait_ge(S.a_land, n2 * len(peers))
+    g.wait_ge(S.a_land, n2 * (len(chips) - 1))
     g.remote_dma_fused(
-        [RemoteDMATransfer(dst_ids=[_dst(topo, r) for r in here], dma_engine_mask=_join(onchip[:R3_ENGINES]),
+        [RemoteDMATransfer(dst_ids=[_dst(topo, r) for r in here], dma_engine_mask=_mask(topo, core, here, ON),
                            remote_sem=S.s_p, srcs=srcs, dsts=[T.p[:, cols] for _ in here], alu_op=1)],
         local_sem=S.a_sent)
-    g.wait_ge(S.a_sent, R0_ENGINES + n2 + R3_ENGINES)
+    g.wait_ge(S.a_sent, ON + n2 + ON)
 
 
 def rank_program(g, core, T, topo):
-    chips, ranks, agents, dies = _plan(T, topo)
+    plan = _plan(T, topo)
     if T.rank_of(core) is not None:
-        _rank(g, core, T, topo, chips, ranks, agents, dies)
-    elif core in agents.values():
-        _agent(g, core, T, topo, chips, ranks, agents, dies)
+        _rank(g, core, T, topo, plan)
+    elif core in plan[2].values() or core in plan[3].values():
+        _helper(g, core, T, topo, plan)

@@ -2,7 +2,11 @@ from concourse.bass import DstId, RemoteDMATransfer
 from concourse.mybir import AluOpType
 
 HALF = 64
+W = 32
+NQ = 4
 ON = 16
+R1 = 8
+AIDED = 2
 
 SCRATCH = {
     "xs": ("sbuf", [128, 128], "float32"),
@@ -23,11 +27,11 @@ SCRATCH = {
     "pr": ("psum", [128, 512], "float32"),
     "py0": ("psum", [128, 512], "float32"),
     "py1": ("psum", [128, 512], "float32"),
-    "pat": ("sbuf", [128, HALF + 1], "float32"),
-    "zero": ("sbuf", [128, HALF], "float32"),
-    "part": ("dram", [2, 128, HALF], "float32"),
-    "land": ("dram", [8, 128, HALF], "float32"),
-    "diag": ("dram", [129, HALF], "float32"),
+    "pat": ("sbuf", [128, W + 1], "float32"),
+    "zero": ("sbuf", [128, W], "float32"),
+    "part": ("dram", [4, 128, W], "float32"),
+    "land": ("dram", [8, 128, W], "float32"),
+    "diag": ("dram", [129, W], "float32"),
 }
 SEMAPHORES = ["s_x", "s_xt", "s_c1", "s_g0", "s_g1", "s_gs0", "s_gs1", "s_i", "s_p", "s_h", "s_q", "s_t", "s_qs",
               "s_x1", "s_r", "s_ss0", "s_ss1", "s_y0", "s_y1", "s_ys0", "s_ys1", "s_st0", "s_st1", "s_sent",
@@ -45,28 +49,36 @@ def _join(bits):
     return m
 
 
-def _mask(topo, src, dsts, n=None):
+def _common(topo, src, dsts):
     m = topo.mask(src, dsts[0])
     for d in dsts:
         m &= topo.mask(src, d)
-    b = _bits(m)
-    return _join(b if n is None else b[:n])
+    return _bits(m)
 
 
 def _plan(T, topo):
     cores = list(T.cores)
     chips = sorted({topo.chip(c) for c in cores})
     ranks = {ch: [c for c in cores if topo.chip(c) == ch] for ch in chips}
-    able = {}
+    able, rest = {}, {}
     for c in range(0, max(cores) + 64):
-        if topo.chip(c) in ranks and all(topo.may_write(c, r) for r in cores if r != c):
-            able.setdefault((topo.chip(c), topo.die(c)), []).append(c)
-    agents, seconds = {}, {}
-    for key, cs in able.items():
+        if topo.chip(c) not in ranks:
+            continue
+        key = (topo.chip(c), topo.die(c))
+        if all(topo.may_write(c, r) for r in cores if r != c):
+            able.setdefault(key, []).append(c)
+        elif c not in cores:
+            rest.setdefault(key, []).append(c)
+    dies = sorted({d for (_, d) in able})
+    send, coll, aide = {}, {}, {}
+    for (ch, d), cs in able.items():
+        u = dies.index(d)
         order = [c for c in cs if c not in cores] + [c for c in cs if c in cores]
-        agents[key], seconds[key] = order[0], order[1]
-    dies = sorted({d for (_, d) in agents})
-    return chips, ranks, agents, seconds, dies
+        aide[(ch, u)] = rest[(ch, d)][-1]
+        for i in range(2):
+            send[(ch, 2 * u + i)] = order[i]
+            coll[(ch, 2 * u + i)] = rest[(ch, d)][0] if order[i] in cores else order[i]
+    return chips, ranks, send, coll, aide
 
 
 def _dst(topo, c):
@@ -74,27 +86,31 @@ def _dst(topo, c):
     return DstId(rid=rid, pnc=pid)
 
 
-def _spread(g, core, T, topo, plan, second, local_sem):
-    chips, ranks, agents, seconds, dies = plan
+def _spread(g, core, T, topo, plan, q, first, by_aide, local_sem):
+    chips, ranks, send, coll, aide = plan
     ch = topo.chip(core)
-    peers = [agents[(c, topo.die(core))] for c in chips if c != ch][(1 if second else 0)::2]
-    m = _mask(topo, core, peers)
+    aided = [c for c in chips if topo.same_plane(ch, c)][-AIDED:]
+    share = [c for c in chips if c != ch and (c in aided) == by_aide]
+    peers = [coll[(c, q)] for c in share]
+    b = _common(topo, core, peers)
     g.remote_dma_fused(
-        [RemoteDMATransfer(dst_ids=[_dst(topo, p) for p in peers], dma_engine_mask=m, remote_sem=T.sem.a_land,
-                           srcs=[T.part[0], T.part[1]], dsts=[T.land[chips.index(ch)] for _ in peers], alu_op=1)],
+        [RemoteDMATransfer(dst_ids=[_dst(topo, p) for p in peers], dma_engine_mask=_join(b),
+                           remote_sem=T.sem.a_land, srcs=[T.part[first], T.part[first + 1]],
+                           dsts=[T.land[chips.index(ch)] for _ in peers], alu_op=1)],
         local_sem=local_sem)
-    return len(_bits(m))
+    return len(b)
 
 
 def _rank(g, core, T, topo, plan):
-    chips, ranks, agents, seconds, dies = plan
+    chips, ranks, send, coll, aide = plan
     S = T.sem
     ch = topo.chip(core)
     slot = ranks[ch].index(core)
     A = slice(0, 128)
     B = slice(0, HALF)
     cols = [slice(HALF * u, HALF * (u + 1)) for u in range(2)]
-    sender = seconds[(ch, topo.die(core))] == core
+    lane = [slice(W * q, W * (q + 1)) for q in range(NQ)]
+    own = [q for q in range(NQ) if send[(ch, q)] == core]
 
     g.sync.dma_start(T.xs[:], T.x[:]).then_inc(S.s_x, 16)
     g.scalar.wait_ge(S.s_x, 16)
@@ -105,31 +121,36 @@ def _rank(g, core, T, topo, plan):
     g.vector.wait_ge(S.s_c1, 1)
     for u in range(2):
         pg = T["pg%d" % u]
-        key = (ch, dies[u])
-        to = [c for c in (agents[key], seconds[key]) if c != core]
         g.tensor.matmul(pg[:, B], T.xs[:], T.xs[:, cols[u]], True, True).then_inc(S["s_g%d" % u], 1)
         g.vector.wait_ge(S["s_g%d" % u], 1)
         g.vector.tensor_tensor(T.gs[:, cols[u]], pg[:, B], T.cm05[:], AluOpType.mult).then_inc(S["s_gs%d" % u], 1)
         g.wait_ge(S["s_gs%d" % u], 1)
-        g.remote_dma_fused(
-            [RemoteDMATransfer(dst_ids=[_dst(topo, c) for c in to], dma_engine_mask=_mask(topo, core, to, ON),
-                               remote_sem=S.a_part, src=T.gs[:, cols[u]], dsts=[T.part[slot] for _ in to])],
-            local_sem=S.s_sent)
-        if len(to) == 1:
-            g.sync.wait_ge(S["s_gs%d" % u], 1)
-            g.sync.dma_start(T.part[slot], T.gs[:, cols[u]]).then_inc(S.s_own, 16)
-    sent = 2 * ON
-    if sender:
+        trs = []
+        for i in range(2):
+            q = 2 * u + i
+            to = sorted({send[(ch, q)], coll[(ch, q)]} - {core})
+            dsts = [T.part[slot] for _ in to] + [T.part[2 * i + slot]]
+            to = to + [aide[(ch, u)]]
+            trs.append(RemoteDMATransfer(dst_ids=[_dst(topo, c) for c in to],
+                                         dma_engine_mask=_join(_common(topo, core, to)[i::2][:R1]),
+                                         remote_sem=S.a_part, src=T.gs[:, lane[q]], dsts=dsts))
+        g.remote_dma_fused(trs, local_sem=S.s_sent)
+        for q in own:
+            if q // 2 == u:
+                g.sync.wait_ge(S["s_gs%d" % u], 1)
+                g.sync.dma_start(T.part[slot], T.gs[:, lane[q]]).then_inc(S.s_own, 16)
+    sent = 4 * R1
+    for q in own:
         g.wait_ge(S.s_own, 16)
-        g.wait_ge(S.a_part, ON)
-        sent += _spread(g, core, T, topo, plan, True, S.s_sent)
+        g.wait_ge(S.a_part, R1)
+        sent += _spread(g, core, T, topo, plan, q, 0, False, S.s_sent)
 
     g.tensor.wait_ge(S.s_xt, 16)
-    g.tensor.wait_ge(S.s_p, 2 * ON)
+    g.tensor.wait_ge(S.s_p, NQ * ON)
     g.tensor.matmul(T.pq[:, A], T.p[:], T.p[:], True, True).then_inc(S.s_q, 1)
     g.tensor.matmul(T.pt[:, A], T.p[:], T.xts[:], True, True).then_inc(S.s_t, 1)
-    g.vector.wait_ge(S.s_i, 2 * ON)
-    g.vector.wait_ge(S.s_p, 2 * ON)
+    g.vector.wait_ge(S.s_i, NQ * ON)
+    g.vector.wait_ge(S.s_p, NQ * ON)
     g.vector.tensor_tensor(T.h[:], T.p[:], T.i15[:], AluOpType.subtract).then_inc(S.s_h, 1)
     g.vector.wait_ge(S.s_q, 1)
     g.vector.tensor_copy(T.qs[:], T.pq[:, A]).then_inc(S.s_qs, 1)
@@ -156,56 +177,70 @@ def _rank(g, core, T, topo, plan):
     g.wait_ge(S.s_sent, sent)
 
 
-def _helper(g, core, T, topo, plan):
-    chips, ranks, agents, seconds, dies = plan
+def _identity(g, core, T, topo, q, to):
     S = T.sem
-    ch = topo.chip(core)
-    key = (ch, topo.die(core))
-    u = dies.index(key[1])
-    ci = chips.index(ch)
-    here = ranks[ch]
-    second = seconds[key] == core
-    cols = slice(HALF * u, HALF * (u + 1))
-
-    g.vector.memset(T.pat[0:HALF, 0:1], 1.5).then_inc(S.a_fill, 1)
-    g.vector.memset(T.pat[0:HALF, 1:HALF + 1], 0.0).then_inc(S.a_fill, 1)
+    g.vector.memset(T.pat[0:W, 0:1], 1.5).then_inc(S.a_fill, 1)
+    g.vector.memset(T.pat[0:W, 1:W + 1], 0.0).then_inc(S.a_fill, 1)
     g.vector.memset(T.zero[:], 0.0).then_inc(S.a_fill, 1)
-    base = HALF * u
+    base = W * q
     g.sync.wait_ge(S.a_fill, 3)
-    g.sync.dma_start(T.diag[base:base + HALF + 1, :], T.pat[0:HALF, :]).then_inc(S.a_d1, 16)
-    lo, hi = (0, base) if u else (HALF + 1, 128)
+    g.sync.dma_start(T.diag[base:base + W + 1, :], T.pat[0:W, :]).then_inc(S.a_d1, 16)
+    gaps = [(lo, hi) for (lo, hi) in ((0, base), (base + W + 1, 128)) if lo < hi]
     g.scalar.wait_ge(S.a_fill, 3)
-    g.scalar.dma_start(T.diag[lo:hi, :], T.zero[0:hi - lo, :]).then_inc(S.a_d2, 16)
-
-    if seconds[key] in here:
-        to = here
-    else:
-        to = here[1:] if second else here[:1]
+    for lo, hi in gaps:
+        g.scalar.dma_start(T.diag[lo:hi, :], T.zero[0:hi - lo, :]).then_inc(S.a_d2, 16)
     g.wait_ge(S.a_d1, 16)
-    g.wait_ge(S.a_d2, 16)
+    g.wait_ge(S.a_d2, 16 * len(gaps))
     g.remote_dma_fused(
-        [RemoteDMATransfer(dst_ids=[_dst(topo, r) for r in to], dma_engine_mask=_mask(topo, core, here, ON),
-                           remote_sem=S.s_i, src=T.diag[0:128, :], dsts=[T.i15[:, cols] for _ in to])],
+        [RemoteDMATransfer(dst_ids=[_dst(topo, r) for r in to], dma_engine_mask=_join(_common(topo, core, to)[:ON]),
+                           remote_sem=S.s_i, src=T.diag[0:128, :],
+                           dsts=[T.i15[:, W * q:W * (q + 1)] for _ in to])],
         local_sem=S.a_sent)
 
-    g.wait_ge(S.a_part, 2 * ON)
-    n2 = _spread(g, core, T, topo, plan, second, S.a_sent)
-    if second:
-        g.wait_ge(S.a_sent, ON + n2)
-        return
 
+def _collector(g, core, T, topo, plan, q):
+    chips, ranks, send, coll, aide = plan
+    S = T.sem
+    ch = topo.chip(core)
+    ci = chips.index(ch)
+    here = ranks[ch]
+    _identity(g, core, T, topo, q, here if q % 2 == 0 else here[:1])
+    sent = ON
+
+    g.wait_ge(S.a_part, 2 * R1)
+    if send[(ch, q)] == core:
+        sent += _spread(g, core, T, topo, plan, q, 0, False, S.a_sent)
+
+    n2 = len(_common(topo, send[(chips[ci - 1], q)], [core]))
     srcs = [T.land[k] for k in range(len(chips)) if k != ci] + [T.part[0], T.part[1], T.diag[0:128, :]]
     g.wait_ge(S.a_land, n2 * (len(chips) - 1))
     g.remote_dma_fused(
-        [RemoteDMATransfer(dst_ids=[_dst(topo, r) for r in here], dma_engine_mask=_mask(topo, core, here, ON),
-                           remote_sem=S.s_p, srcs=srcs, dsts=[T.p[:, cols] for _ in here], alu_op=1)],
+        [RemoteDMATransfer(dst_ids=[_dst(topo, r) for r in here],
+                           dma_engine_mask=_join(_common(topo, core, here)[:ON]), remote_sem=S.s_p,
+                           srcs=srcs, dsts=[T.p[:, W * q:W * (q + 1)] for _ in here], alu_op=1)],
         local_sem=S.a_sent)
-    g.wait_ge(S.a_sent, ON + n2 + ON)
+    g.wait_ge(S.a_sent, sent + ON)
+
+
+def _aide(g, core, T, topo, plan, u):
+    S = T.sem
+    here = plan[1][topo.chip(core)]
+    _identity(g, core, T, topo, 2 * u + 1, here[1:])
+    sent = ON
+    g.wait_ge(S.a_part, 4 * R1)
+    for i in range(2):
+        sent += _spread(g, core, T, topo, plan, 2 * u + i, 2 * i, True, S.a_sent)
+    g.wait_ge(S.a_sent, sent)
 
 
 def rank_program(g, core, T, topo):
     plan = _plan(T, topo)
     if T.rank_of(core) is not None:
         _rank(g, core, T, topo, plan)
-    elif core in plan[2].values() or core in plan[3].values():
-        _helper(g, core, T, topo, plan)
+        return
+    for (ch, q), c in plan[3].items():
+        if c == core:
+            _collector(g, core, T, topo, plan, q)
+    for (ch, u), c in plan[4].items():
+        if c == core:
+            _aide(g, core, T, topo, plan, u)

@@ -7,35 +7,39 @@ NQ = 4
 ON = 16
 R1 = 8
 AIDED = 2
+CA1, CA0 = 2.25, 0.84375
+CM1, CM0 = 1.078125, 1.5380859375
 
 SCRATCH = {
+    "cst": ("sbuf", [128, 128], "float32"),
+    "e1": ("sbuf", [128, 128], "float32"),
     "xs": ("sbuf", [128, 128], "float32"),
     "xts": ("sbuf", [128, 128], "float32"),
+    "xc": ("sbuf", [128, 128], "float32"),
     "cm05": ("sbuf", [128, HALF], "float32"),
     "gs": ("sbuf", [128, 128], "float32"),
-    "i15": ("sbuf", [128, 128], "float32"),
-    "p": ("sbuf", [128, 128], "float32"),
     "h": ("sbuf", [128, 128], "float32"),
-    "qs": ("sbuf", [128, 128], "float32"),
-    "x1t": ("sbuf", [128, 128], "float32"),
-    "ss": ("sbuf", [128, 128], "float32"),
+    "hk": ("sbuf", [128, 128], "float32"),
+    "c1": ("sbuf", [128, 128], "float32"),
+    "c2": ("sbuf", [128, 128], "float32"),
+    "a": ("sbuf", [128, 128], "float32"),
+    "m": ("sbuf", [128, 128], "float32"),
     "ys": ("sbuf", [128, 128], "float32"),
     "pg0": ("psum", [128, 512], "float32"),
     "pg1": ("psum", [128, 512], "float32"),
-    "pq": ("psum", [128, 512], "float32"),
-    "pt": ("psum", [128, 512], "float32"),
-    "pr": ("psum", [128, 512], "float32"),
+    "pq0": ("psum", [128, 512], "float32"),
+    "pq1": ("psum", [128, 512], "float32"),
+    "pt0": ("psum", [128, 512], "float32"),
+    "pt1": ("psum", [128, 512], "float32"),
     "py0": ("psum", [128, 512], "float32"),
     "py1": ("psum", [128, 512], "float32"),
-    "pat": ("sbuf", [128, W + 1], "float32"),
-    "zero": ("sbuf", [128, W], "float32"),
     "part": ("dram", [4, 128, W], "float32"),
     "land": ("dram", [8, 128, W], "float32"),
-    "diag": ("dram", [129, W], "float32"),
 }
-SEMAPHORES = ["s_x", "s_xt", "s_c1", "s_g0", "s_g1", "s_gs0", "s_gs1", "s_i", "s_p", "s_h", "s_q", "s_t", "s_qs",
-              "s_x1", "s_r", "s_ss0", "s_ss1", "s_y0", "s_y1", "s_ys0", "s_ys1", "s_st0", "s_st1", "s_sent",
-              "s_own", "a_fill", "a_d1", "a_d2", "a_part", "a_land", "a_sent"]
+SEMAPHORES = ["s_x", "s_xt", "s_c1", "s_g0", "s_g1", "s_gs0", "s_gs1", "s_xc", "s_i", "s_p", "s_q0", "s_q1",
+              "s_k0", "s_k1", "s_d0", "s_d1", "s_a0", "s_a1", "s_c2", "s_t0", "s_t1", "s_m0", "s_m1",
+              "s_y0", "s_y1", "s_ys0", "s_ys1", "s_st0", "s_st1", "s_sent", "s_own",
+              "a_fill", "a_sel", "a_part", "a_land", "a_sent"]
 
 
 def _bits(m):
@@ -60,10 +64,11 @@ def _plan(T, topo):
     cores = list(T.cores)
     chips = sorted({topo.chip(c) for c in cores})
     ranks = {ch: [c for c in cores if topo.chip(c) == ch] for ch in chips}
-    able, rest = {}, {}
+    able, rest, every = {}, {}, {}
     for c in range(0, max(cores) + 64):
         if topo.chip(c) not in ranks:
             continue
+        every.setdefault(topo.chip(c), []).append(c)
         key = (topo.chip(c), topo.die(c))
         if all(topo.may_write(c, r) for r in cores if r != c):
             able.setdefault(key, []).append(c)
@@ -78,7 +83,7 @@ def _plan(T, topo):
         for i in range(2):
             send[(ch, 2 * u + i)] = order[i]
             coll[(ch, 2 * u + i)] = rest[(ch, d)][0] if order[i] in cores else order[i]
-    return chips, ranks, send, coll, aide
+    return chips, ranks, send, coll, aide, every
 
 
 def _dst(topo, c):
@@ -86,11 +91,32 @@ def _dst(topo, c):
     return DstId(rid=rid, pnc=pid)
 
 
+def _unit(g, core, T, topo, plan, local_sem):
+    S = T.sem
+    ch = topo.chip(core)
+    mine = plan[5][ch]
+    w = 128 // len(mine)
+    k = mine.index(core)
+    cols = slice(w * k, w * (k + 1))
+    to = [r for r in plan[1][ch] if r != core]
+    g.vector.memset(T.cst[:, 0:w], CA0).then_inc(S.a_fill, 1)
+    g.wait_ge(S.a_fill, 1)
+    g.affine_select(T.e1[:, cols], T.cst[:, 0:w], [[-1, w]], AluOpType.is_equal, 0.0, -w * k, 1).then_inc(S.a_sel, 1)
+    g.wait_ge(S.a_sel, 1)
+    g.remote_dma_fused(
+        [RemoteDMATransfer(dst_ids=[_dst(topo, r) for r in to], dma_engine_mask=_join(_common(topo, core, to)[:ON]),
+                           remote_sem=S.s_i, src=T.e1[:, cols], dsts=[T.e1[:, cols] for _ in to])],
+        local_sem=local_sem)
+    return ON
+
+
 def _spread(g, core, T, topo, plan, q, first, by_aide, local_sem):
-    chips, ranks, send, coll, aide = plan
+    chips, send, coll = plan[0], plan[2], plan[3]
     ch = topo.chip(core)
     aided = [c for c in chips if topo.same_plane(ch, c)][-AIDED:]
     share = [c for c in chips if c != ch and (c in aided) == by_aide]
+    if by_aide and coll[(ch, q)] != send[(ch, q)]:
+        share = share + [ch]
     peers = [coll[(c, q)] for c in share]
     b = _common(topo, core, peers)
     g.remote_dma_fused(
@@ -102,19 +128,18 @@ def _spread(g, core, T, topo, plan, q, first, by_aide, local_sem):
 
 
 def _rank(g, core, T, topo, plan):
-    chips, ranks, send, coll, aide = plan
+    chips, ranks, send, coll, aide, every = plan
     S = T.sem
     ch = topo.chip(core)
     slot = ranks[ch].index(core)
-    A = slice(0, 128)
     B = slice(0, HALF)
     cols = [slice(HALF * u, HALF * (u + 1)) for u in range(2)]
     lane = [slice(W * q, W * (q + 1)) for q in range(NQ)]
     own = [q for q in range(NQ) if send[(ch, q)] == core]
+    mult, add = AluOpType.mult, AluOpType.add
 
     g.sync.dma_start(T.xs[:], T.x[:]).then_inc(S.s_x, 16)
-    g.scalar.wait_ge(S.s_x, 16)
-    g.scalar.dma_start(T.xts[:], T.xt[:]).then_inc(S.s_xt, 16)
+    sent = _unit(g, core, T, topo, plan, S.s_sent)
     g.vector.memset(T.cm05[:], -0.5).then_inc(S.s_c1, 1)
 
     g.tensor.wait_ge(S.s_x, 16)
@@ -123,12 +148,12 @@ def _rank(g, core, T, topo, plan):
         pg = T["pg%d" % u]
         g.tensor.matmul(pg[:, B], T.xs[:], T.xs[:, cols[u]], True, True).then_inc(S["s_g%d" % u], 1)
         g.vector.wait_ge(S["s_g%d" % u], 1)
-        g.vector.tensor_tensor(T.gs[:, cols[u]], pg[:, B], T.cm05[:], AluOpType.mult).then_inc(S["s_gs%d" % u], 1)
+        g.vector.tensor_tensor(T.gs[:, cols[u]], pg[:, B], T.cm05[:], mult).then_inc(S["s_gs%d" % u], 1)
         g.wait_ge(S["s_gs%d" % u], 1)
         trs = []
         for i in range(2):
             q = 2 * u + i
-            to = sorted({send[(ch, q)], coll[(ch, q)]} - {core})
+            to = [c for c in [send[(ch, q)]] if c != core]
             dsts = [T.part[slot] for _ in to] + [T.part[2 * i + slot]]
             to = to + [aide[(ch, u)]]
             trs.append(RemoteDMATransfer(dst_ids=[_dst(topo, c) for c in to],
@@ -139,94 +164,90 @@ def _rank(g, core, T, topo, plan):
             if q // 2 == u:
                 g.sync.wait_ge(S["s_gs%d" % u], 1)
                 g.sync.dma_start(T.part[slot], T.gs[:, lane[q]]).then_inc(S.s_own, 16)
-    sent = 4 * R1
+    sent += 4 * R1
     for q in own:
         g.wait_ge(S.s_own, 16)
         g.wait_ge(S.a_part, R1)
         sent += _spread(g, core, T, topo, plan, q, 0, False, S.s_sent)
+    g.scalar.wait_ge(S.s_sent, sent)
+    g.scalar.dma_start(T.xts[:], T.xt[:]).then_inc(S.s_xt, 16)
+    g.vector.wait_ge(S.s_x, 16)
+    g.vector.tensor_scalar(T.xc[:], T.xs[:], CM0, None, mult).then_inc(S.s_xc, 1)
 
-    g.tensor.wait_ge(S.s_xt, 16)
-    g.tensor.wait_ge(S.s_p, NQ * ON)
-    g.tensor.matmul(T.pq[:, A], T.p[:], T.p[:], True, True).then_inc(S.s_q, 1)
-    g.tensor.matmul(T.pt[:, A], T.p[:], T.xts[:], True, True).then_inc(S.s_t, 1)
-    g.vector.wait_ge(S.s_i, NQ * ON)
-    g.vector.wait_ge(S.s_p, NQ * ON)
-    g.vector.tensor_tensor(T.h[:], T.p[:], T.i15[:], AluOpType.subtract).then_inc(S.s_h, 1)
-    g.vector.wait_ge(S.s_q, 1)
-    g.vector.tensor_copy(T.qs[:], T.pq[:, A]).then_inc(S.s_qs, 1)
-    g.vector.wait_ge(S.s_t, 1)
-    g.vector.tensor_copy(T.x1t[:], T.pt[:, A]).then_inc(S.s_x1, 1)
-    g.tensor.wait_ge(S.s_h, 1)
-    g.tensor.wait_ge(S.s_qs, 1)
-    g.tensor.matmul(T.pr[:, A], T.qs[:], T.h[:], True, True).then_inc(S.s_r, 1)
-    g.vector.wait_ge(S.s_r, 1)
+    landed = NQ * ON
+    g.tensor.wait_ge(S.s_p, landed)
     for u in range(2):
-        g.vector.tensor_tensor(T.ss[:, cols[u]], T.pr[:, cols[u]], T.i15[:, cols[u]],
-                               AluOpType.add).then_inc(S["s_ss%d" % u], 1)
-    g.tensor.wait_ge(S.s_x1, 1)
+        g.tensor.matmul(T["pq%d" % u][:, B], T.h[:], T.h[:, cols[u]], True, True).then_inc(S["s_q%d" % u], 1)
+    g.vector.wait_ge(S.a_sel, 1)
+    g.vector.wait_ge(S.s_i, ON * (len(every[ch]) - 1))
+    g.vector.wait_ge(S.s_p, landed)
+    g.vector.tensor_scalar(T.hk[:, cols[0]], T.h[:, cols[0]], CA1, None, mult).then_inc(S.s_k0, 1)
+    g.vector.wait_ge(S.s_k0, 1)
+    g.vector.tensor_tensor(T.c1[:, cols[0]], T.hk[:, cols[0]], T.e1[:, cols[0]], add).then_inc(S.s_d0, 1)
+    g.vector.tensor_scalar(T.hk[:, cols[1]], T.h[:, cols[1]], CA1, None, mult).then_inc(S.s_k1, 1)
+    g.vector.wait_ge(S.s_d0, 1)
+    g.vector.wait_ge(S.s_q0, 1)
+    g.vector.tensor_tensor(T.a[:, cols[0]], T.pq0[:, B], T.c1[:, cols[0]], add).then_inc(S.s_a0, 1)
+    g.vector.wait_ge(S.s_k1, 1)
+    g.vector.tensor_tensor(T.c1[:, cols[1]], T.hk[:, cols[1]], T.e1[:, cols[1]], add).then_inc(S.s_d1, 1)
+    g.vector.wait_ge(S.s_d1, 1)
+    g.vector.wait_ge(S.s_q1, 1)
+    g.vector.tensor_tensor(T.a[:, cols[1]], T.pq1[:, B], T.c1[:, cols[1]], add).then_inc(S.s_a1, 1)
+    g.vector.tensor_scalar(T.c2[:], T.h[:], CM1, None, mult).then_inc(S.s_c2, 1)
+    g.tensor.wait_ge(S.s_a0, 1)
+    g.tensor.wait_ge(S.s_a1, 1)
+    for u in range(2):
+        g.tensor.matmul(T["pt%d" % u][:, B], T.a[:], T.a[:, cols[u]], True, True).then_inc(S["s_t%d" % u], 1)
+    g.vector.wait_ge(S.s_c2, 1)
+    for u in range(2):
+        g.vector.wait_ge(S["s_t%d" % u], 1)
+        g.vector.tensor_tensor(T.m[:, cols[u]], T["pt%d" % u][:, B], T.c2[:, cols[u]],
+                               add).then_inc(S["s_m%d" % u], 1)
+    g.tensor.wait_ge(S.s_xt, 16)
+    g.vector.wait_ge(S.s_xc, 1)
     queues = [g.sync, g.scalar]
     for u in range(2):
         py = T["py%d" % u]
-        g.tensor.wait_ge(S["s_ss%d" % u], 1)
-        g.tensor.matmul(py[:, B], T.x1t[:], T.ss[:, cols[u]], True, True).then_inc(S["s_y%d" % u], 1)
+        g.tensor.wait_ge(S["s_m%d" % u], 1)
+        g.tensor.matmul(py[:, B], T.xts[:], T.m[:, cols[u]], True, True).then_inc(S["s_y%d" % u], 1)
         g.vector.wait_ge(S["s_y%d" % u], 1)
-        g.vector.tensor_copy(T.ys[:, cols[u]], py[:, B]).then_inc(S["s_ys%d" % u], 1)
+        g.vector.tensor_tensor(T.ys[:, cols[u]], py[:, B], T.xc[:, cols[u]], add).then_inc(S["s_ys%d" % u], 1)
         queues[u].wait_ge(S["s_ys%d" % u], 1)
         queues[u].dma_start(T.y[:, cols[u]], T.ys[:, cols[u]]).then_inc(S["s_st%d" % u], 16)
         queues[u].wait_ge(S["s_st%d" % u], 16)
     g.wait_ge(S.s_sent, sent)
 
 
-def _identity(g, core, T, topo, q, to):
-    S = T.sem
-    g.vector.memset(T.pat[0:W, 0:1], 1.5).then_inc(S.a_fill, 1)
-    g.vector.memset(T.pat[0:W, 1:W + 1], 0.0).then_inc(S.a_fill, 1)
-    g.vector.memset(T.zero[:], 0.0).then_inc(S.a_fill, 1)
-    base = W * q
-    g.sync.wait_ge(S.a_fill, 3)
-    g.sync.dma_start(T.diag[base:base + W + 1, :], T.pat[0:W, :]).then_inc(S.a_d1, 16)
-    gaps = [(lo, hi) for (lo, hi) in ((0, base), (base + W + 1, 128)) if lo < hi]
-    g.scalar.wait_ge(S.a_fill, 3)
-    for lo, hi in gaps:
-        g.scalar.dma_start(T.diag[lo:hi, :], T.zero[0:hi - lo, :]).then_inc(S.a_d2, 16)
-    g.wait_ge(S.a_d1, 16)
-    g.wait_ge(S.a_d2, 16 * len(gaps))
-    g.remote_dma_fused(
-        [RemoteDMATransfer(dst_ids=[_dst(topo, r) for r in to], dma_engine_mask=_join(_common(topo, core, to)[:ON]),
-                           remote_sem=S.s_i, src=T.diag[0:128, :],
-                           dsts=[T.i15[:, W * q:W * (q + 1)] for _ in to])],
-        local_sem=S.a_sent)
-
-
 def _collector(g, core, T, topo, plan, q):
-    chips, ranks, send, coll, aide = plan
+    chips, ranks, send = plan[0], plan[1], plan[2]
     S = T.sem
     ch = topo.chip(core)
     ci = chips.index(ch)
     here = ranks[ch]
-    _identity(g, core, T, topo, q, here if q % 2 == 0 else here[:1])
-    sent = ON
+    sent = _unit(g, core, T, topo, plan, S.a_sent)
 
-    g.wait_ge(S.a_part, 2 * R1)
     if send[(ch, q)] == core:
+        g.wait_ge(S.a_part, 2 * R1)
         sent += _spread(g, core, T, topo, plan, q, 0, False, S.a_sent)
+        srcs = [T.land[k] for k in range(len(chips)) if k != ci] + [T.part[0], T.part[1]]
+        lands = len(chips) - 1
+    else:
+        srcs = [T.land[k] for k in range(len(chips))]
+        lands = len(chips)
 
     n2 = len(_common(topo, send[(chips[ci - 1], q)], [core]))
-    srcs = [T.land[k] for k in range(len(chips)) if k != ci] + [T.part[0], T.part[1], T.diag[0:128, :]]
-    g.wait_ge(S.a_land, n2 * (len(chips) - 1))
+    g.wait_ge(S.a_land, n2 * lands)
     g.remote_dma_fused(
         [RemoteDMATransfer(dst_ids=[_dst(topo, r) for r in here],
                            dma_engine_mask=_join(_common(topo, core, here)[:ON]), remote_sem=S.s_p,
-                           srcs=srcs, dsts=[T.p[:, W * q:W * (q + 1)] for _ in here], alu_op=1)],
+                           srcs=srcs, dsts=[T.h[:, W * q:W * (q + 1)] for _ in here], alu_op=1)],
         local_sem=S.a_sent)
     g.wait_ge(S.a_sent, sent + ON)
 
 
 def _aide(g, core, T, topo, plan, u):
     S = T.sem
-    here = plan[1][topo.chip(core)]
-    _identity(g, core, T, topo, 2 * u + 1, here[1:])
-    sent = ON
+    sent = _unit(g, core, T, topo, plan, S.a_sent)
     g.wait_ge(S.a_part, 4 * R1)
     for i in range(2):
         sent += _spread(g, core, T, topo, plan, 2 * u + i, 2 * i, True, S.a_sent)

from concourse.bass import DstId, RemoteDMATransfer
from concourse.mybir import AluOpType

HALF = 64
W = 32
NQ = 4
ON = 16
R1 = 8
AIDED = 2
CA1, CA0 = 2.25, 0.84375
CM1, CM0 = 1.078125, 1.5380859375

SCRATCH = {
    "cst": ("sbuf", [128, 128], "float32"),
    "e1": ("sbuf", [128, 128], "float32"),
    "xs": ("sbuf", [128, 128], "float32"),
    "xts": ("sbuf", [128, 128], "float32"),
    "xc": ("sbuf", [128, 128], "float32"),
    "cm05": ("sbuf", [128, HALF], "float32"),
    "gs": ("sbuf", [128, 128], "float32"),
    "h": ("sbuf", [128, 128], "float32"),
    "hk": ("sbuf", [128, 128], "float32"),
    "c1": ("sbuf", [128, 128], "float32"),
    "c2": ("sbuf", [128, 128], "float32"),
    "a": ("sbuf", [128, 128], "float32"),
    "m": ("sbuf", [128, 128], "float32"),
    "ys": ("sbuf", [128, 128], "float32"),
    "pg0": ("psum", [128, 512], "float32"),
    "pg1": ("psum", [128, 512], "float32"),
    "pq0": ("psum", [128, 512], "float32"),
    "pq1": ("psum", [128, 512], "float32"),
    "pt0": ("psum", [128, 512], "float32"),
    "pt1": ("psum", [128, 512], "float32"),
    "py0": ("psum", [128, 512], "float32"),
    "py1": ("psum", [128, 512], "float32"),
    "part": ("dram", [4, 128, W], "float32"),
    "land": ("dram", [8, 128, W], "float32"),
}
SEMAPHORES = ["s_x", "s_xt", "s_c1", "s_g0", "s_g1", "s_gs0", "s_gs1", "s_xc", "s_i", "s_p", "s_q0", "s_q1",
              "s_k0", "s_k1", "s_d0", "s_d1", "s_a0", "s_a1", "s_c2", "s_t0", "s_t1", "s_m0", "s_m1",
              "s_y0", "s_y1", "s_ys0", "s_ys1", "s_st0", "s_st1", "s_sent", "s_own",
              "a_fill", "a_sel", "a_part", "a_land", "a_sent"]


def _bits(m):
    return [1 << i for i in range(m.bit_length()) if (m >> i) & 1]


def _join(bits):
    m = 0
    for b in bits:
        m |= b
    return m


def _common(topo, src, dsts):
    m = topo.mask(src, dsts[0])
    for d in dsts:
        m &= topo.mask(src, d)
    return _bits(m)


def _plan(T, topo):
    cores = list(T.cores)
    chips = sorted({topo.chip(c) for c in cores})
    ranks = {ch: [c for c in cores if topo.chip(c) == ch] for ch in chips}
    able, rest, every = {}, {}, {}
    for c in range(0, max(cores) + 64):
        if topo.chip(c) not in ranks:
            continue
        every.setdefault(topo.chip(c), []).append(c)
        key = (topo.chip(c), topo.die(c))
        if all(topo.may_write(c, r) for r in cores if r != c):
            able.setdefault(key, []).append(c)
        elif c not in cores:
            rest.setdefault(key, []).append(c)
    dies = sorted({d for (_, d) in able})
    send, coll, aide = {}, {}, {}
    for (ch, d), cs in able.items():
        u = dies.index(d)
        order = [c for c in cs if c not in cores] + [c for c in cs if c in cores]
        aide[(ch, u)] = rest[(ch, d)][-1]
        for i in range(2):
            send[(ch, 2 * u + i)] = order[i]
            coll[(ch, 2 * u + i)] = rest[(ch, d)][0] if order[i] in cores else order[i]
    return chips, ranks, send, coll, aide, every


def _dst(topo, c):
    rid, pid, _ = topo.addr(c)
    return DstId(rid=rid, pnc=pid)


def _unit(g, core, T, topo, plan, local_sem):
    S = T.sem
    ch = topo.chip(core)
    mine = plan[5][ch]
    w = 128 // len(mine)
    k = mine.index(core)
    cols = slice(w * k, w * (k + 1))
    to = [r for r in plan[1][ch] if r != core]
    g.vector.memset(T.cst[:, 0:w], CA0).then_inc(S.a_fill, 1)
    g.wait_ge(S.a_fill, 1)
    g.affine_select(T.e1[:, cols], T.cst[:, 0:w], [[-1, w]], AluOpType.is_equal, 0.0, -w * k, 1).then_inc(S.a_sel, 1)
    g.wait_ge(S.a_sel, 1)
    g.remote_dma_fused(
        [RemoteDMATransfer(dst_ids=[_dst(topo, r) for r in to], dma_engine_mask=_join(_common(topo, core, to)[:ON]),
                           remote_sem=S.s_i, src=T.e1[:, cols], dsts=[T.e1[:, cols] for _ in to])],
        local_sem=local_sem)
    return ON


def _spread(g, core, T, topo, plan, q, first, by_aide, local_sem):
    chips, send, coll = plan[0], plan[2], plan[3]
    ch = topo.chip(core)
    aided = [c for c in chips if topo.same_plane(ch, c)][-AIDED:]
    share = [c for c in chips if c != ch and (c in aided) == by_aide]
    if by_aide and coll[(ch, q)] != send[(ch, q)]:
        share = share + [ch]
    peers = [coll[(c, q)] for c in share]
    b = _common(topo, core, peers)
    g.remote_dma_fused(
        [RemoteDMATransfer(dst_ids=[_dst(topo, p) for p in peers], dma_engine_mask=_join(b),
                           remote_sem=T.sem.a_land, srcs=[T.part[first], T.part[first + 1]],
                           dsts=[T.land[chips.index(ch)] for _ in peers], alu_op=1)],
        local_sem=local_sem)
    return len(b)


def _rank(g, core, T, topo, plan):
    chips, ranks, send, coll, aide, every = plan
    S = T.sem
    ch = topo.chip(core)
    slot = ranks[ch].index(core)
    B = slice(0, HALF)
    cols = [slice(HALF * u, HALF * (u + 1)) for u in range(2)]
    lane = [slice(W * q, W * (q + 1)) for q in range(NQ)]
    own = [q for q in range(NQ) if send[(ch, q)] == core]
    mult, add = AluOpType.mult, AluOpType.add

    g.sync.dma_start(T.xs[:], T.x[:]).then_inc(S.s_x, 16)
    sent = _unit(g, core, T, topo, plan, S.s_sent)
    g.vector.memset(T.cm05[:], -0.5).then_inc(S.s_c1, 1)

    g.tensor.wait_ge(S.s_x, 16)
    g.vector.wait_ge(S.s_c1, 1)
    for u in range(2):
        pg = T["pg%d" % u]
        g.tensor.matmul(pg[:, B], T.xs[:], T.xs[:, cols[u]], True, True).then_inc(S["s_g%d" % u], 1)
        g.vector.wait_ge(S["s_g%d" % u], 1)
        g.vector.tensor_tensor(T.gs[:, cols[u]], pg[:, B], T.cm05[:], mult).then_inc(S["s_gs%d" % u], 1)
        g.wait_ge(S["s_gs%d" % u], 1)
        trs = []
        for i in range(2):
            q = 2 * u + i
            to = [c for c in [send[(ch, q)]] if c != core]
            dsts = [T.part[slot] for _ in to] + [T.part[2 * i + slot]]
            to = to + [aide[(ch, u)]]
            trs.append(RemoteDMATransfer(dst_ids=[_dst(topo, c) for c in to],
                                         dma_engine_mask=_join(_common(topo, core, to)[i::2][:R1]),
                                         remote_sem=S.a_part, src=T.gs[:, lane[q]], dsts=dsts))
        g.remote_dma_fused(trs, local_sem=S.s_sent)
        for q in own:
            if q // 2 == u:
                g.sync.wait_ge(S["s_gs%d" % u], 1)
                g.sync.dma_start(T.part[slot], T.gs[:, lane[q]]).then_inc(S.s_own, 16)
    sent += 4 * R1
    for q in own:
        g.wait_ge(S.s_own, 16)
        g.wait_ge(S.a_part, R1)
        sent += _spread(g, core, T, topo, plan, q, 0, False, S.s_sent)
    g.scalar.wait_ge(S.s_sent, sent)
    g.scalar.dma_start(T.xts[:], T.xt[:]).then_inc(S.s_xt, 16)
    g.vector.wait_ge(S.s_x, 16)
    g.vector.tensor_scalar(T.xc[:], T.xs[:], CM0, None, mult).then_inc(S.s_xc, 1)

    landed = NQ * ON
    g.tensor.wait_ge(S.s_p, landed)
    for u in range(2):
        g.tensor.matmul(T["pq%d" % u][:, B], T.h[:], T.h[:, cols[u]], True, True).then_inc(S["s_q%d" % u], 1)
    g.vector.wait_ge(S.a_sel, 1)
    g.vector.wait_ge(S.s_i, ON * (len(every[ch]) - 1))
    g.vector.wait_ge(S.s_p, landed)
    g.vector.tensor_scalar(T.hk[:, cols[0]], T.h[:, cols[0]], CA1, None, mult).then_inc(S.s_k0, 1)
    g.vector.wait_ge(S.s_k0, 1)
    g.vector.tensor_tensor(T.c1[:, cols[0]], T.hk[:, cols[0]], T.e1[:, cols[0]], add).then_inc(S.s_d0, 1)
    g.vector.tensor_scalar(T.hk[:, cols[1]], T.h[:, cols[1]], CA1, None, mult).then_inc(S.s_k1, 1)
    g.vector.wait_ge(S.s_d0, 1)
    g.vector.wait_ge(S.s_q0, 1)
    g.vector.tensor_tensor(T.a[:, cols[0]], T.pq0[:, B], T.c1[:, cols[0]], add).then_inc(S.s_a0, 1)
    g.vector.wait_ge(S.s_k1, 1)
    g.vector.tensor_tensor(T.c1[:, cols[1]], T.hk[:, cols[1]], T.e1[:, cols[1]], add).then_inc(S.s_d1, 1)
    g.vector.wait_ge(S.s_d1, 1)
    g.vector.wait_ge(S.s_q1, 1)
    g.vector.tensor_tensor(T.a[:, cols[1]], T.pq1[:, B], T.c1[:, cols[1]], add).then_inc(S.s_a1, 1)
    g.vector.tensor_scalar(T.c2[:], T.h[:], CM1, None, mult).then_inc(S.s_c2, 1)
    g.tensor.wait_ge(S.s_a0, 1)
    g.tensor.wait_ge(S.s_a1, 1)
    for u in range(2):
        g.tensor.matmul(T["pt%d" % u][:, B], T.a[:], T.a[:, cols[u]], True, True).then_inc(S["s_t%d" % u], 1)
    g.vector.wait_ge(S.s_c2, 1)
    for u in range(2):
        g.vector.wait_ge(S["s_t%d" % u], 1)
        g.vector.tensor_tensor(T.m[:, cols[u]], T["pt%d" % u][:, B], T.c2[:, cols[u]],
                               add).then_inc(S["s_m%d" % u], 1)
    g.tensor.wait_ge(S.s_xt, 16)
    g.vector.wait_ge(S.s_xc, 1)
    queues = [g.sync, g.scalar]
    for u in range(2):
        py = T["py%d" % u]
        g.tensor.wait_ge(S["s_m%d" % u], 1)
        g.tensor.matmul(py[:, B], T.xts[:], T.m[:, cols[u]], True, True).then_inc(S["s_y%d" % u], 1)
        g.vector.wait_ge(S["s_y%d" % u], 1)
        g.vector.tensor_tensor(T.ys[:, cols[u]], py[:, B], T.xc[:, cols[u]], add).then_inc(S["s_ys%d" % u], 1)
        queues[u].wait_ge(S["s_ys%d" % u], 1)
        queues[u].dma_start(T.y[:, cols[u]], T.ys[:, cols[u]]).then_inc(S["s_st%d" % u], 16)
        queues[u].wait_ge(S["s_st%d" % u], 16)
    g.wait_ge(S.s_sent, sent)


def _collector(g, core, T, topo, plan, q):
    chips, ranks, send = plan[0], plan[1], plan[2]
    S = T.sem
    ch = topo.chip(core)
    ci = chips.index(ch)
    here = ranks[ch]
    sent = _unit(g, core, T, topo, plan, S.a_sent)

    if send[(ch, q)] == core:
        g.wait_ge(S.a_part, 2 * R1)
        sent += _spread(g, core, T, topo, plan, q, 0, False, S.a_sent)
        srcs = [T.land[k] for k in range(len(chips)) if k != ci] + [T.part[0], T.part[1]]
        lands = len(chips) - 1
    else:
        srcs = [T.land[k] for k in range(len(chips))]
        lands = len(chips)

    n2 = len(_common(topo, send[(chips[ci - 1], q)], [core]))
    g.wait_ge(S.a_land, n2 * lands)
    g.remote_dma_fused(
        [RemoteDMATransfer(dst_ids=[_dst(topo, r) for r in here],
                           dma_engine_mask=_join(_common(topo, core, here)[:ON]), remote_sem=S.s_p,
                           srcs=srcs, dsts=[T.h[:, W * q:W * (q + 1)] for _ in here], alu_op=1)],
        local_sem=S.a_sent)
    g.wait_ge(S.a_sent, sent + ON)


def _aide(g, core, T, topo, plan, u):
    S = T.sem
    sent = _unit(g, core, T, topo, plan, S.a_sent)
    g.wait_ge(S.a_part, 4 * R1)
    for i in range(2):
        sent += _spread(g, core, T, topo, plan, 2 * u + i, 2 * i, True, S.a_sent)
    g.wait_ge(S.a_sent, sent)


def rank_program(g, core, T, topo):
    plan = _plan(T, topo)
    if T.rank_of(core) is not None:
        _rank(g, core, T, topo, plan)
        return
    for (ch, q), c in plan[3].items():
        if c == core:
            _collector(g, core, T, topo, plan, q)
    for (ch, u), c in plan[4].items():
        if c == core:
            _aide(g, core, T, topo, plan, u)
